import numpy as np
import ml_dtypes


def mxq(x, axis, fmt="e4m3"):
    dtype, down = {"e4m3": (ml_dtypes.float8_e4m3fn, 7), "e5m2": (ml_dtypes.float8_e5m2, 14)}[fmt]
    v = np.moveaxis(np.asarray(x, np.float32).astype(ml_dtypes.bfloat16).astype(np.float64), axis, -1)
    blocks = v.reshape(v.shape[:-1] + (-1, 32))
    amax = np.abs(blocks).max(-1, keepdims=True)
    byte = np.maximum(np.where(amax > 0, np.frexp(amax)[1] - 1 + 127, 0) - down, 1)
    scale = np.exp2(byte - 127.0)
    codes = (blocks / scale).astype(np.float32).astype(dtype).astype(np.float64)
    return np.moveaxis((codes * scale).reshape(v.shape), -1, axis)


WIDE = False


def mx_kscale(k):
    if not WIDE:
        return np.ones(k)
    levels = np.array([10, -10, 5, -5, 0])
    if k % 512:
        return np.exp2(np.random.permutation(np.resize(levels, k // 32))).repeat(32)
    a = np.empty((k // 512, 16))
    for p in range(k // 512):
        a[p, :8] = np.random.permutation(np.resize(levels, 8))
        for g in range(8):
            far = levels[np.abs(levels - a[p, g]) >= 10]
            a[p, g + 8] = far[np.random.randint(len(far))]
    return np.exp2(a.ravel()).repeat(32)


def f64(x):
    return np.asarray(x).astype(np.float64)


def striped(idx):
    return np.tile(idx.reshape(-1, 16).T, (8, 1)).astype(np.uint16)


def unstriped(offs):
    return offs[:16].T.reshape(-1).astype(np.int64)


E2M1 = np.array([0.0, 0.5, 1.0, 1.5, 2.0, 3.0, 4.0, 6.0, -0.0, -0.5, -1.0, -1.5, -2.0, -3.0, -4.0, -6.0])


def pack_weight(w, fmt):
    k, n = w.shape
    w = f64(np.asarray(w, np.float32).astype(ml_dtypes.bfloat16)).reshape(k // 32, 32, n)
    amax = np.abs(w).max(1)
    if fmt == "e4m3":
        byte = np.frexp(amax)[1] - 1 + 127 - 7
    else:
        mant, ex = np.frexp(amax / 6.0)
        byte = np.where(mant > 0.5, ex, ex - 1) + 127
    byte = np.clip(np.where(amax > 0, byte, 1), 1, 254)
    scaled = (w * np.exp2(127.0 - byte)[:, None, :]).reshape(k, n).astype(np.float32)
    by_word = np.ascontiguousarray(scaled.reshape(k // 512, 128, 4, n).transpose(0, 1, 3, 2))
    if fmt == "e4m3":
        words = by_word.astype(ml_dtypes.float8_e4m3fn).view(np.uint8)
    else:
        c = by_word.astype(ml_dtypes.float4_e2m1fn).view(np.uint8) & 0xF
        words = (c[..., 0::2] | (c[..., 1::2] << 4)).reshape(k // 512, 128, 2 * n)
    return np.ascontiguousarray(words), np.ascontiguousarray(byte.astype(np.uint8).reshape(k // 512, 16, n))


def unpack_weight(words, scales, fmt):
    g, _, n = scales.shape
    words = np.ascontiguousarray(words).reshape(g, 128, n, -1)
    if fmt == "e4m3":
        vals = words.view(ml_dtypes.float8_e4m3fn).astype(np.float64)
    else:
        nib = np.empty((g, 128, n, 4), np.uint8)
        nib[..., 0::2] = words & 0xF
        nib[..., 1::2] = words >> 4
        vals = E2M1[nib]
    vals = vals * np.repeat(np.exp2(scales.astype(np.float64) - 127.0), 8, axis=1)[..., None]
    return vals.transpose(0, 1, 3, 2).reshape(g * 512, n)


def gelu(v):
    return 0.5 * v * (1.0 + np.tanh(np.sqrt(2.0 / np.pi) * (v + 0.044715 * v**3)))


K, T, S, H, T2, P, N = 1024, 4096, 1024, 512, 2048, 1024, 384

def setup_inputs():
    n = np.random.standard_normal
    s = mx_kscale(K)[:, None]
    u = mx_kscale(H)[:, None]
    d = {}
    d["tab_words"], d["tab_scales"] = pack_weight(n((K, T)) * s, "e4m3")
    d["offs"] = striped(np.random.permutation(T)[:S])
    d["wa"] = (n((K, H)) / s / K ** 0.5).astype(np.float32)
    d["wb_words"], d["wb_scales"] = pack_weight(n((K, H)) / s / K ** 0.5, "e2m1")
    d["wc"] = (n((K, H)) / s / K ** 0.5).astype(np.float32)
    d["gain"] = (np.exp(0.3 * n(H)) * u[:, 0]).astype(np.float32)
    d["wgs"] = np.exp(0.3 * n((128, S))).astype(np.float32)
    d["page0"] = (n((H, T2)) * u).astype(np.float32)
    d["offs2"] = striped(np.random.permutation(T2)[:S])
    d["offs3"] = striped(np.random.permutation(T2)[:P])
    d["base"] = (0.5 * n(H) * u[:, 0]).astype(np.float32)
    d["w4_words"], d["w4_scales"] = pack_weight(n((H, N)) / u / H ** 0.5, "e4m3")
    d["thr"] = (0.7 * n(N)).astype(np.float32)
    d["wgo"] = np.exp(0.3 * n((128, P))).astype(np.float32)
    d["page1"] = n((N, T2)).astype(np.float32)
    d["offs4"] = striped(np.random.permutation(T2)[:P])
    return d

def reference(tab_words, tab_scales, offs, wa, wb_words, wb_scales, wc, gain, wgs, page0, offs2, offs3, base, w4_words, w4_scales, thr, wgo, page1, offs4):
    v = unpack_weight(tab_words, tab_scales, "e4m3")[:, unstriped(offs)]
    a = mxq(f64(wa), 0, "e4m3").T @ v
    b = unpack_weight(wb_words, wb_scales, "e2m1").T @ v
    c = mxq(f64(wc), 0, "e4m3").T @ v
    h = np.tanh(c + a * b) * f64(gain)[:, None]
    page = f64(page0).copy()
    page[:, unstriped(offs2)] = np.tile(f64(wgs), (H // 128, 1)) * h
    x = np.maximum(page[:, unstriped(offs3)], f64(base)[:, None])
    x8 = mxq(x, 0, "e4m3")
    y = np.abs((unpack_weight(w4_words, w4_scales, "e4m3").T @ x8) - f64(thr)[:, None])
    out = f64(page1).copy()
    out[:, unstriped(offs4)] = np.tile(f64(wgo), (N // 128, 1)) * y
    return out

@@ -1,0 +1,280 @@
+from contextlib import ExitStack
+
+import concourse.mybir as mybir
+from concourse.masks import make_identity
+
+K, T, S, H, T2, PICK, N = 1024, 4096, 1024, 512, 2048, 1024, 384
+FLOPS = 2 * (3 * K * H * S + H * N * PICK)
+
+F32 = mybir.dt.float32
+BF16 = mybir.dt.bfloat16
+I32 = mybir.dt.int32
+U32 = mybir.dt.uint32
+U16 = mybir.dt.uint16
+U8 = mybir.dt.uint8
+FP8X4 = mybir.dt.float8_e4m3fn_x4
+FP4X4 = mybir.dt.float4_e2m1fn_x4
+ACT = mybir.ActivationFunctionType
+ALU = mybir.AluOpType
+
+P = 128
+PASSES = K // 512
+ROW_BLOCKS = H // P
+OUT_BLOCKS = N // P
+HALF = 512
+LIST_COLS = HALF // 16
+JB = HALF // P
+
+
+def tile_list_latex_tapping_roster_kernel(
+    tc, tab_words, tab_scales, offs, wa, wb_words, wb_scales, wc, gain, wgs, page0, offs2, offs3,
+    base, w4_words, w4_scales, thr, wgo, page1, offs4, out,
+):
+    nc = tc.nc
+    with ExitStack() as ctx:
+        lists = ctx.enter_context(tc.tile_pool(name="lists", bufs=1))
+        keep = ctx.enter_context(tc.tile_pool(name="keep", bufs=1))
+        ring = ctx.enter_context(tc.tile_pool(name="ring", bufs=2))
+        psum = ctx.enter_context(tc.psum_pool(name="psum", bufs=1))
+
+        def held(name, shape, dtype):
+            return keep.tile(shape, dtype, name=name, align_bytes=64)
+
+        def bank(name):
+            return psum.tile([P, HALF], F32, name=name, tag="acc", bufs=4)
+
+        def half_list(tile, half):
+            return tile[:, half * LIST_COLS : (half + 1) * LIST_COLS]
+
+        idx = lists.tile([P, S // 16], U16, name="idx")
+        idx2 = lists.tile([P, S // 16], U16, name="idx2")
+        idx3 = lists.tile([P, PICK // 16], U16, name="idx3")
+        idx4 = lists.tile([P, PICK // 16], U16, name="idx4")
+
+        wb_planes = held("wb_planes", [P, PASSES, H], U8)
+        nc.vector.memset(wb_planes[:].rearrange("p a c -> p (a c)").bitcast(I32), 0)
+        tab_planes = held("tab_planes", [P, T], U8)
+        for q in range(4):
+            nc.vector.memset(tab_planes[32 * q : 32 * q + 24, :].bitcast(I32), 0)
+        v_plane = [held(f"v_plane{a}", [P, S], U8) for a in range(PASSES)]
+        for a in range(PASSES):
+            nc.vector.memset(v_plane[a][96:P, :].bitcast(I32), 0)
+        vec_rows = held("vec_rows", [P, P], F32)
+        nc.gpsimd.memset(vec_rows[:], 0.0)
+        ident = held("ident", [P, P], F32)
+        make_identity(nc, ident[:])
+        w4_plane = held("w4_plane", [P, N], U8)
+        nc.vector.memset(w4_plane[:].bitcast(I32), 0)
+
+        warm = held("warm", [P, 1], F32)
+        nc.scalar.activation(warm[:], vec_rows[:, 0:1], ACT.Tanh)
+
+        for q in range(4):
+            nc.gpsimd.dma_start(
+                wb_planes[32 * q : 32 * q + 4, :, :].bitcast(I32),
+                wb_scales[:, 4 * q : 4 * q + 4, :].rearrange("a r c -> r a c").bitcast(I32),
+            )
+
+        nc.sync.dma_start(idx[:], offs)
+        for q in range(4):
+            nc.sync.dma_start(
+                tab_planes[32 * q + 24 : 32 * q + 32, :].bitcast(I32),
+                tab_scales[:, 4 * q : 4 * q + 4, :].bitcast(I32),
+            )
+        table = [held(f"table{a}", [P, T], U32) for a in range(PASSES)]
+        raw = [[held(f"raw{u}_{a}", [P, 2, 4, P], F32) for a in range(PASSES)] for u in range(ROW_BLOCKS)]
+        pages = [held(f"page{u}", [P, T2], F32) for u in range(ROW_BLOCKS)]
+        outs = [held(f"out{n}", [P, T2], F32) for n in range(OUT_BLOCKS)]
+
+        def load_table(a):
+            nc.sync.dma_start(table[a][:].bitcast(I32), tab_words[a].rearrange("p t i -> p (t i)").bitcast(I32))
+
+        def load_weights(u):
+            for a in range(PASSES):
+                for w, weight in enumerate((wa, wc)):
+                    rows = weight[512 * a : 512 * (a + 1), P * u : P * (u + 1)]
+                    nc.sync.dma_start(raw[u][a][:, w], rows.rearrange("(p j) c -> p j c", j=4))
+
+        load_table(0)
+        load_weights(0)
+        wb_codes = held("wb_codes", [P, PASSES, 2 * H], U8)
+        nc.sync.dma_start(wb_codes[:].bitcast(I32), wb_words.rearrange("a p c -> p a c").bitcast(I32))
+        nc.sync.dma_start(vec_rows[0:4, :], gain.rearrange("(u p) -> u p", p=P))
+        nc.sync.dma_start(vec_rows[4:8, :], base.rearrange("(u p) -> u p", p=P))
+        nc.sync.dma_start(vec_rows[8:11, :], thr.rearrange("(u p) -> u p", p=P))
+        load_table(1)
+        nc.sync.dma_start(pages[0][:], page0[0:P, :])
+        wgs_sb = held("wgs_sb", [P, S], F32)
+        nc.sync.dma_start(wgs_sb[:], wgs)
+        nc.sync.dma_start(idx2[:], offs2)
+        nc.sync.dma_start(idx3[:], offs3)
+        for u in range(1, ROW_BLOCKS):
+            load_weights(u)
+            nc.sync.dma_start(pages[u][:], page0[P * u : P * (u + 1), :])
+        w4_codes = held("w4_codes", [P, N], U32)
+        nc.sync.dma_start(w4_codes[:].bitcast(I32), w4_words[0].rearrange("p c i -> p (c i)").bitcast(I32))
+        for q in range(4):
+            nc.sync.dma_start(
+                w4_plane[32 * q : 32 * q + 4, :].bitcast(I32),
+                w4_scales[0, 4 * q : 4 * q + 4, :].bitcast(I32),
+            )
+        nc.sync.dma_start(idx4[:], offs4)
+        wgo_sb = held("wgo_sb", [P, PICK], F32)
+        nc.sync.dma_start(wgo_sb[:], wgo)
+        for n in range(OUT_BLOCKS):
+            nc.sync.dma_start(outs[n][:], page1[P * n : P * (n + 1), :])
+
+        v_planes = held("v_planes", [P, S], U8)
+        nc.vector.tensor_copy(v_planes[:], tab_planes[:].indirect(idx[:]))
+        for a in range(PASSES):
+            nc.gpsimd.dma_start(v_plane[a][0:100, :].bitcast(I32), v_planes[24 + 4 * a : 124 + 4 * a, :].bitcast(I32))
+
+        ident_bf = held("ident_bf", [P, P], BF16)
+        make_identity(nc, ident_bf[:])
+        vec_bank = bank("vec_bank")
+        nc.tensor.transpose(vec_bank[:, 0:P], vec_rows[:], ident[:])
+        vec = held("vec", [P, 16], F32)
+        nc.scalar.copy(vec[:], vec_bank[:, 0:16])
+
+        v_codes = [[held(f"v_codes{a}_{h}", [P, HALF], U32) for h in range(2)] for a in range(PASSES)]
+
+        def gather_table(a, half):
+            nc.vector.tensor_copy(v_codes[a][half][:], table[a][:].indirect(half_list(idx, half)))
+
+        w_codes = [[held(f"w_codes{u}_{a}", [P, 2 * P], U32) for a in range(PASSES)] for u in range(ROW_BLOCKS)]
+        w_plane = [[held(f"w_plane{u}_{a}", [P, 2 * P], U8) for a in range(PASSES)] for u in range(ROW_BLOCKS)]
+
+        def quantise_weights(u):
+            for a in range(PASSES):
+                grouped = ring.tile([P, 2, P, 4], BF16, name="grouped", align_bytes=64, bufs=3)
+                dst = grouped[:].rearrange("p w (c i) j -> p w c j i", i=4)
+                src = raw[u][a][:].rearrange("p w j (c i) -> p w c j i", i=4)
+                if u == 0:
+                    nc.vector.tensor_copy(dst, src)
+                else:
+                    nc.scalar.copy(dst, src)
+                nc.vector.quantize_mx(
+                    out=w_codes[u][a][:].bitcast(FP8X4),
+                    scales=w_plane[u][a][:],
+                    in_=grouped[:].rearrange("p w c j -> p (w c j)"),
+                )
+
+        wg = [held(f"wg{s}", [P, S], F32) for s in range(2)]
+        hs = [held(f"h{s}", [P, HALF], F32) for s in range(2)]
+
+        def scale_wgs(u):
+            nc.scalar.activation(wg[u % 2][:], wgs_sb[:], ACT.Copy, scale=vec[:, u : u + 1])
+
+        def products(u, half):
+            ac = [bank("ac") for pair in range(2)]
+            b_bank = psum.tile([P, JB, P], F32, name="b_bank", bufs=2)
+            for a in range(PASSES):
+                for jb in range(JB):
+                    cols = slice(P * jb, P * (jb + 1))
+                    lhs = v_codes[a][half][:, cols].bitcast(FP8X4)
+                    lhs_scale = v_plane[a][:, HALF * half + P * jb : HALF * half + P * (jb + 1)]
+                    nc.tensor.matmul_mx(
+                        out=ac[jb // 2][:, 2 * P * (jb % 2) : 2 * P * (jb % 2 + 1)],
+                        lhsT=lhs, lhsT_scale=lhs_scale,
+                        rhs=w_codes[u][a][:].bitcast(FP8X4), rhs_scale=w_plane[u][a][:],
+                        start=(a == 0 and jb % 2 == 0), stop=(a == PASSES - 1 and jb % 2 == 1),
+                    )
+                    nc.tensor.matmul_mx(
+                        out=b_bank[:, jb, :],
+                        lhsT=lhs, lhsT_scale=lhs_scale,
+                        rhs=wb_codes[:, a, 2 * P * u : 2 * P * (u + 1)].bitcast(FP4X4),
+                        rhs_scale=wb_planes[:, a, P * u : P * (u + 1)],
+                        start=(a == 0 and jb == 0), stop=(a == PASSES - 1 and jb == JB - 1),
+                    )
+            ac_sb = ring.tile([P, JB, 2, P], F32, name="ac_sb")
+            for pair in range(2):
+                nc.scalar.copy(ac_sb[:, 2 * pair : 2 * pair + 2].rearrange("p b w r -> p (b w r)"), ac[pair][:])
+            ab = ring.tile([P, JB, P], F32, name="ab")
+            nc.vector.tensor_tensor(ab[:], b_bank[:], ac_sb[:, :, 0, :], ALU.mult)
+            return ac_sb, ab
+
+        def put_states(u, half, ac_sb, ab):
+            total = psum.tile([P, JB, P], F32, name="total")
+            for jb in range(JB):
+                nc.tensor.matmul(total[:, jb, :], ac_sb[:, jb, 1, :], ident[:], start=(jb == 0), stop=False, is_transpose=True)
+            for jb in range(JB):
+                nc.tensor.matmul(total[:, jb, :], ab[:, jb, :], ident[:], start=False, stop=(jb == JB - 1), is_transpose=True)
+            nc.scalar.activation(hs[half][:], total[:].rearrange("p b r -> p (b r)"), ACT.Tanh)
+            nc.vector.tensor_tensor(
+                pages[u][:].indirect(half_list(idx2, half)),
+                hs[half][:], wg[u % 2][:, HALF * half : HALF * (half + 1)], ALU.mult,
+            )
+
+        x_t = [held(f"x_t{h}", [P, JB, H], BF16) for h in range(2)]
+
+        def recall(u, half, picked):
+            nc.vector.tensor_copy(picked, pages[u][:].indirect(half_list(idx3, half)))
+            lifted = ring.tile([P, HALF], BF16, name="lifted")
+            nc.vector.tensor_scalar(lifted[:], picked, vec[:, 4 + u : 5 + u], None, ALU.max)
+            turned = psum.tile([P, JB, P], BF16, name="turned")
+            for jb in range(JB):
+                nc.tensor.transpose(turned[:, jb, :], lifted[:, P * jb : P * (jb + 1)], ident_bf[:])
+            nc.scalar.copy(x_t[half][:, :, P * u : P * (u + 1)], turned[:])
+
+        def quantise_x(half):
+            x_grouped = ring.tile([P, 4 * HALF], BF16, name="x_grouped", align_bytes=64)
+            x_words = x_grouped[:].bitcast(F32)
+            for pair in range(2):
+                back = bank("back")
+                for b in range(2):
+                    words = x_t[half][:, 2 * pair + b, :].bitcast(F32)
+                    for e in range(2):
+                        nc.tensor.transpose(back[:, P * (2 * b + e) : P * (2 * b + e + 1)], words[:, e : 2 * P : 2], ident[:])
+                nc.scalar.copy(
+                    x_words[:, HALF * pair : HALF * (pair + 1)].rearrange("p (b j e) -> p b j e", b=2, e=2),
+                    back[:].rearrange("p (b e j) -> p b j e", b=2, e=2),
+                )
+            x_codes = ring.tile([P, HALF], U32, name="x_codes", align_bytes=64)
+            x_plane = ring.tile([P, HALF], U8, name="x_plane", align_bytes=64)
+            nc.vector.quantize_mx(out=x_codes[:].bitcast(FP8X4), scales=x_plane[:], in_=x_grouped[:])
+            return x_codes, x_plane
+
+        def put_features(half, x_codes, x_plane):
+            for n in range(OUT_BLOCKS):
+                y_bank = bank("y_bank")
+                nc.tensor.matmul_mx(
+                    out=y_bank[:],
+                    lhsT=w4_codes[:, P * n : P * (n + 1)].bitcast(FP8X4), lhsT_scale=w4_plane[:, P * n : P * (n + 1)],
+                    rhs=x_codes[:].bitcast(FP8X4), rhs_scale=x_plane[:],
+                    start=True, stop=True,
+                )
+                y = ring.tile([P, HALF], F32, name="y", bufs=3)
+                nc.scalar.activation(y[:], y_bank[:], ACT.Abs, bias=vec[:, 8 + n : 9 + n], scale=-1.0)
+                nc.vector.tensor_tensor(
+                    outs[n][:].indirect(half_list(idx4, half)),
+                    y[:], wgo_sb[:, HALF * half : HALF * (half + 1)], ALU.mult,
+                )
+                if half == 1:
+                    nc.sync.dma_start(out[P * n : P * (n + 1), :], outs[n][:])
+
+        gather_table(0, 0)
+        gather_table(0, 1)
+        quantise_weights(0)
+        gather_table(1, 0)
+        gather_table(1, 1)
+        steps = [(u, half) for u in range(ROW_BLOCKS) for half in range(2)]
+        ahead = products(*steps[0])
+        for i, (u, half) in enumerate(steps):
+            now = ahead
+            if half == 0:
+                scale_wgs(u)
+            if i + 1 < len(steps):
+                if half == 1:
+                    quantise_weights(u + 1)
+                ahead = products(*steps[i + 1])
+            put_states(u, half, *now)
+            if half == 1:
+                picked = ring.tile([P, HALF], F32, name="picked")
+                recall(u, 0, picked[:])
+
+        x_first = quantise_x(0)
+        late = [hs[1][:], wg[1][:, HALF:S]]
+        for u in range(ROW_BLOCKS):
+            recall(u, 1, late[u % 2])
+        put_features(0, *x_first)
+        put_features(1, *quantise_x(1))

@@ -40,8 +40,7 @@ def tile_list_latex_tapping_roster_kernel(
         def held(name, shape, dtype):
             return keep.tile(shape, dtype, name=name, align_bytes=64)
 
-        def bank(name):
-            return psum.tile([P, HALF], F32, name=name, tag="acc", bufs=4)
+        banks = [psum.tile([P, HALF], F32, name=f"bank{i}") for i in range(4)]
 
         def half_list(tile, half):
             return tile[:, half * LIST_COLS : (half + 1) * LIST_COLS]
@@ -51,36 +50,23 @@ def tile_list_latex_tapping_roster_kernel(
         idx3 = lists.tile([P, PICK // 16], U16, name="idx3")
         idx4 = lists.tile([P, PICK // 16], U16, name="idx4")
 
+        tab_planes = held("tab_planes", [P, T], U8)
+        nc.vector.memset(tab_planes[:].bitcast(I32), 0)
         wb_planes = held("wb_planes", [P, PASSES, H], U8)
         nc.vector.memset(wb_planes[:].rearrange("p a c -> p (a c)").bitcast(I32), 0)
-        tab_planes = held("tab_planes", [P, T], U8)
-        for q in range(4):
-            nc.vector.memset(tab_planes[32 * q : 32 * q + 24, :].bitcast(I32), 0)
-        v_plane = [held(f"v_plane{a}", [P, S], U8) for a in range(PASSES)]
-        for a in range(PASSES):
-            nc.vector.memset(v_plane[a][96:P, :].bitcast(I32), 0)
-        vec_rows = held("vec_rows", [P, P], F32)
-        nc.gpsimd.memset(vec_rows[:], 0.0)
+        v_plane1 = [held(f"v_plane1_{h}", [P, HALF], U8) for h in range(2)]
+        for h in range(2):
+            nc.vector.memset(v_plane1[h][96:P, :].bitcast(I32), 0)
         ident = held("ident", [P, P], F32)
         make_identity(nc, ident[:])
         w4_plane = held("w4_plane", [P, N], U8)
         nc.vector.memset(w4_plane[:].bitcast(I32), 0)
 
         warm = held("warm", [P, 1], F32)
-        nc.scalar.activation(warm[:], vec_rows[:, 0:1], ACT.Tanh)
+        nc.scalar.activation(warm[:], ident[:, 0:1], ACT.Tanh)
 
-        for q in range(4):
-            nc.gpsimd.dma_start(
-                wb_planes[32 * q : 32 * q + 4, :, :].bitcast(I32),
-                wb_scales[:, 4 * q : 4 * q + 4, :].rearrange("a r c -> r a c").bitcast(I32),
-            )
 
         nc.sync.dma_start(idx[:], offs)
-        for q in range(4):
-            nc.sync.dma_start(
-                tab_planes[32 * q + 24 : 32 * q + 32, :].bitcast(I32),
-                tab_scales[:, 4 * q : 4 * q + 4, :].bitcast(I32),
-            )
         table = [held(f"table{a}", [P, T], U32) for a in range(PASSES)]
         raw = [[held(f"raw{u}_{a}", [P, 2, 4, P], F32) for a in range(PASSES)] for u in range(ROW_BLOCKS)]
         pages = [held(f"page{u}", [P, T2], F32) for u in range(ROW_BLOCKS)]
@@ -96,21 +82,42 @@ def tile_list_latex_tapping_roster_kernel(
                     nc.sync.dma_start(raw[u][a][:, w], rows.rearrange("(p j) c -> p j c", j=4))
 
         load_table(0)
+        for q in range(4):
+            nc.sync.dma_start(
+                tab_planes[32 * q : 32 * q + 8, :].bitcast(I32),
+                tab_scales[:, 4 * q : 4 * q + 4, :].bitcast(I32),
+            )
         load_weights(0)
+        load_table(1)
         wb_codes = held("wb_codes", [P, PASSES, 2 * H], U8)
         nc.sync.dma_start(wb_codes[:].bitcast(I32), wb_words.rearrange("a p c -> p a c").bitcast(I32))
-        nc.sync.dma_start(vec_rows[0:4, :], gain.rearrange("(u p) -> u p", p=P))
-        nc.sync.dma_start(vec_rows[4:8, :], base.rearrange("(u p) -> u p", p=P))
-        nc.sync.dma_start(vec_rows[8:11, :], thr.rearrange("(u p) -> u p", p=P))
-        load_table(1)
-        nc.sync.dma_start(pages[0][:], page0[0:P, :])
-        wgs_sb = held("wgs_sb", [P, S], F32)
-        nc.sync.dma_start(wgs_sb[:], wgs)
+        for q in range(4):
+            nc.sync.dma_start(
+                wb_planes[32 * q : 32 * q + 4, :, :].bitcast(I32),
+                wb_scales[:, 4 * q : 4 * q + 4, :].rearrange("a r c -> r a c").bitcast(I32),
+            )
+
+        def load_columns(name, vector, first, count):
+            tile = held(name, [P, count], F32)
+            with nc.allow_non_contiguous_dma(reason="one value of a short vector for each partition"):
+                nc.sync.dma_start(tile[:], vector.rearrange("(u p) -> p u", p=P)[:, first : first + count])
+            return [tile[:, u : u + 1] for u in range(count)]
+
+        gain_col = load_columns("gain_first", gain, 0, 1)
+        wgs_sb = [held(f"wgs{h}", [P, HALF], F32) for h in range(2)]
+        nc.sync.dma_start(wgs_sb[0][:], wgs[:, 0:HALF])
         nc.sync.dma_start(idx2[:], offs2)
+        nc.sync.dma_start(pages[0][:], page0[0:P, :])
+        nc.sync.dma_start(wgs_sb[1][:], wgs[:, HALF:S])
+        load_weights(1)
         nc.sync.dma_start(idx3[:], offs3)
-        for u in range(1, ROW_BLOCKS):
+        gain_col = gain_col + load_columns("gain_rest", gain, 1, ROW_BLOCKS - 1)
+        base_col = load_columns("base_cols", base, 0, ROW_BLOCKS)
+        nc.sync.dma_start(pages[1][:], page0[P : 2 * P, :])
+        for u in range(2, ROW_BLOCKS):
             load_weights(u)
             nc.sync.dma_start(pages[u][:], page0[P * u : P * (u + 1), :])
+        thr_col = load_columns("thr_cols", thr, 0, OUT_BLOCKS)
         w4_codes = held("w4_codes", [P, N], U32)
         nc.sync.dma_start(w4_codes[:].bitcast(I32), w4_words[0].rearrange("p c i -> p (c i)").bitcast(I32))
         for q in range(4):
@@ -124,17 +131,15 @@ def tile_list_latex_tapping_roster_kernel(
         for n in range(OUT_BLOCKS):
             nc.sync.dma_start(outs[n][:], page1[P * n : P * (n + 1), :])
 
-        v_planes = held("v_planes", [P, S], U8)
-        nc.vector.tensor_copy(v_planes[:], tab_planes[:].indirect(idx[:]))
-        for a in range(PASSES):
-            nc.gpsimd.dma_start(v_plane[a][0:100, :].bitcast(I32), v_planes[24 + 4 * a : 124 + 4 * a, :].bitcast(I32))
+        v_planes = [held(f"v_planes{h}", [P, HALF], U8) for h in range(2)]
+        v_plane = [v_planes, v_plane1]
+
+        def gather_scales(half):
+            nc.vector.tensor_copy(v_planes[half][:], tab_planes[:].indirect(half_list(idx, half)))
+            nc.scalar.dma_start(v_plane1[half][0:112, :].bitcast(I32), v_planes[half][4:116, :].bitcast(I32))
 
         ident_bf = held("ident_bf", [P, P], BF16)
         make_identity(nc, ident_bf[:])
-        vec_bank = bank("vec_bank")
-        nc.tensor.transpose(vec_bank[:, 0:P], vec_rows[:], ident[:])
-        vec = held("vec", [P, 16], F32)
-        nc.scalar.copy(vec[:], vec_bank[:, 0:16])
 
         v_codes = [[held(f"v_codes{a}_{h}", [P, HALF], U32) for h in range(2)] for a in range(PASSES)]
 
@@ -159,50 +164,59 @@ def tile_list_latex_tapping_roster_kernel(
                     in_=grouped[:].rearrange("p w c j -> p (w c j)"),
                 )
 
-        wg = [held(f"wg{s}", [P, S], F32) for s in range(2)]
+        wg = [[held(f"wg{s}_{h}", [P, HALF], F32) for h in range(2)] for s in range(2)]
         hs = [held(f"h{s}", [P, HALF], F32) for s in range(2)]
 
-        def scale_wgs(u):
-            nc.scalar.activation(wg[u % 2][:], wgs_sb[:], ACT.Copy, scale=vec[:, u : u + 1])
+        def scale_wgs(u, half):
+            nc.scalar.activation(wg[u % 2][half][:], wgs_sb[half][:], ACT.Copy, scale=gain_col[u])
 
         def products(u, half):
-            ac = [bank("ac") for pair in range(2)]
+            ac = banks[2 * half : 2 * half + 2]
             b_bank = psum.tile([P, JB, P], F32, name="b_bank", bufs=2)
+
+            def entries(a, jb):
+                cols = slice(P * jb, P * (jb + 1))
+                return v_codes[a][half][:, cols].bitcast(FP8X4), cols
+
             for a in range(PASSES):
                 for jb in range(JB):
-                    cols = slice(P * jb, P * (jb + 1))
-                    lhs = v_codes[a][half][:, cols].bitcast(FP8X4)
-                    lhs_scale = v_plane[a][:, HALF * half + P * jb : HALF * half + P * (jb + 1)]
+                    lhs, cols = entries(a, jb)
                     nc.tensor.matmul_mx(
                         out=ac[jb // 2][:, 2 * P * (jb % 2) : 2 * P * (jb % 2 + 1)],
-                        lhsT=lhs, lhsT_scale=lhs_scale,
+                        lhsT=lhs, lhsT_scale=v_planes[half][4 * a : P, cols],
                         rhs=w_codes[u][a][:].bitcast(FP8X4), rhs_scale=w_plane[u][a][:],
                         start=(a == 0 and jb % 2 == 0), stop=(a == PASSES - 1 and jb % 2 == 1),
                     )
+            for a in range(PASSES):
+                for jb in range(JB):
+                    lhs, cols = entries(a, jb)
                     nc.tensor.matmul_mx(
                         out=b_bank[:, jb, :],
-                        lhsT=lhs, lhsT_scale=lhs_scale,
+                        lhsT=lhs, lhsT_scale=v_plane[a][half][:, cols],
                         rhs=wb_codes[:, a, 2 * P * u : 2 * P * (u + 1)].bitcast(FP4X4),
                         rhs_scale=wb_planes[:, a, P * u : P * (u + 1)],
                         start=(a == 0 and jb == 0), stop=(a == PASSES - 1 and jb == JB - 1),
                     )
-            ac_sb = ring.tile([P, JB, 2, P], F32, name="ac_sb")
+            ac_sb = ring.tile([P, 2, JB, P], F32, name="ac_sb", bufs=3)
             for pair in range(2):
-                nc.scalar.copy(ac_sb[:, 2 * pair : 2 * pair + 2].rearrange("p b w r -> p (b w r)"), ac[pair][:])
+                nc.scalar.copy(
+                    ac_sb[:, :, 2 * pair : 2 * pair + 2, :],
+                    ac[pair][:].rearrange("p (b w r) -> p w b r", b=2, w=2),
+                )
             ab = ring.tile([P, JB, P], F32, name="ab")
-            nc.vector.tensor_tensor(ab[:], b_bank[:], ac_sb[:, :, 0, :], ALU.mult)
+            nc.vector.tensor_tensor(ab[:], b_bank[:], ac_sb[:, 0], ALU.mult)
             return ac_sb, ab
 
-        def put_states(u, half, ac_sb, ab):
+        def put_states(u, half, state, ac_sb, ab):
             total = psum.tile([P, JB, P], F32, name="total")
             for jb in range(JB):
-                nc.tensor.matmul(total[:, jb, :], ac_sb[:, jb, 1, :], ident[:], start=(jb == 0), stop=False, is_transpose=True)
+                nc.tensor.matmul(total[:, jb, :], ac_sb[:, 1, jb, :], ident[:], start=(jb == 0), stop=False, is_transpose=True)
             for jb in range(JB):
                 nc.tensor.matmul(total[:, jb, :], ab[:, jb, :], ident[:], start=False, stop=(jb == JB - 1), is_transpose=True)
-            nc.scalar.activation(hs[half][:], total[:].rearrange("p b r -> p (b r)"), ACT.Tanh)
+            nc.scalar.activation(state, total[:].rearrange("p b r -> p (b r)"), ACT.Tanh)
             nc.vector.tensor_tensor(
                 pages[u][:].indirect(half_list(idx2, half)),
-                hs[half][:], wg[u % 2][:, HALF * half : HALF * (half + 1)], ALU.mult,
+                state, wg[u % 2][half][:], ALU.mult,
             )
 
         x_t = [held(f"x_t{h}", [P, JB, H], BF16) for h in range(2)]
@@ -210,7 +224,7 @@ def tile_list_latex_tapping_roster_kernel(
         def recall(u, half, picked):
             nc.vector.tensor_copy(picked, pages[u][:].indirect(half_list(idx3, half)))
             lifted = ring.tile([P, HALF], BF16, name="lifted")
-            nc.vector.tensor_scalar(lifted[:], picked, vec[:, 4 + u : 5 + u], None, ALU.max)
+            nc.vector.tensor_scalar(lifted[:], picked, base_col[u], None, ALU.max)
             turned = psum.tile([P, JB, P], BF16, name="turned")
             for jb in range(JB):
                 nc.tensor.transpose(turned[:, jb, :], lifted[:, P * jb : P * (jb + 1)], ident_bf[:])
@@ -220,7 +234,7 @@ def tile_list_latex_tapping_roster_kernel(
             x_grouped = ring.tile([P, 4 * HALF], BF16, name="x_grouped", align_bytes=64)
             x_words = x_grouped[:].bitcast(F32)
             for pair in range(2):
-                back = bank("back")
+                back = banks[pair]
                 for b in range(2):
                     words = x_t[half][:, 2 * pair + b, :].bitcast(F32)
                     for e in range(2):
@@ -232,11 +246,10 @@ def tile_list_latex_tapping_roster_kernel(
             x_codes = ring.tile([P, HALF], U32, name="x_codes", align_bytes=64)
             x_plane = ring.tile([P, HALF], U8, name="x_plane", align_bytes=64)
             nc.vector.quantize_mx(out=x_codes[:].bitcast(FP8X4), scales=x_plane[:], in_=x_grouped[:])
-            return x_codes, x_plane
+            return x_words, (x_codes, x_plane)
 
-        def put_features(half, x_codes, x_plane):
-            for n in range(OUT_BLOCKS):
-                y_bank = bank("y_bank")
+        def put_features(half, blocks, x_codes, x_plane):
+            for n, y_bank in blocks:
                 nc.tensor.matmul_mx(
                     out=y_bank[:],
                     lhsT=w4_codes[:, P * n : P * (n + 1)].bitcast(FP8X4), lhsT_scale=w4_plane[:, P * n : P * (n + 1)],
@@ -244,7 +257,7 @@ def tile_list_latex_tapping_roster_kernel(
                     start=True, stop=True,
                 )
                 y = ring.tile([P, HALF], F32, name="y", bufs=3)
-                nc.scalar.activation(y[:], y_bank[:], ACT.Abs, bias=vec[:, 8 + n : 9 + n], scale=-1.0)
+                nc.scalar.activation(y[:], y_bank[:], ACT.Abs, bias=thr_col[n], scale=-1.0)
                 nc.vector.tensor_tensor(
                     outs[n][:].indirect(half_list(idx4, half)),
                     y[:], wgo_sb[:, HALF * half : HALF * (half + 1)], ALU.mult,
@@ -252,8 +265,9 @@ def tile_list_latex_tapping_roster_kernel(
                 if half == 1:
                     nc.sync.dma_start(out[P * n : P * (n + 1), :], outs[n][:])
 
-        gather_table(0, 0)
-        gather_table(0, 1)
+        for half in range(2):
+            gather_scales(half)
+            gather_table(0, half)
         quantise_weights(0)
         gather_table(1, 0)
         gather_table(1, 1)
@@ -261,20 +275,26 @@ def tile_list_latex_tapping_roster_kernel(
         ahead = products(*steps[0])
         for i, (u, half) in enumerate(steps):
             now = ahead
-            if half == 0:
-                scale_wgs(u)
-            if i + 1 < len(steps):
-                if half == 1:
-                    quantise_weights(u + 1)
+            scale_wgs(u, half)
+            last = i + 1 == len(steps)
+            takes_weights = u + 1 < ROW_BLOCKS and half == (1 if u == 0 else 0)
+            if takes_weights:
+                quantise_weights(u + 1)
+            if not last:
                 ahead = products(*steps[i + 1])
-            put_states(u, half, *now)
+            if takes_weights:
+                state = raw[u + 1][1][:, 0].rearrange("p j c -> p (j c)")
+            else:
+                state = hs[half][:]
+            put_states(u, half, state, *now)
             if half == 1:
-                picked = ring.tile([P, HALF], F32, name="picked")
-                recall(u, 0, picked[:])
+                recall(u, 0, hs[0][:] if last else ahead[0][:, 0].rearrange("p b r -> p (b r)"))
 
-        x_first = quantise_x(0)
-        late = [hs[1][:], wg[1][:, HALF:S]]
+        spent, x_first = quantise_x(0)
+        late = [hs[1][:], wg[1][1][:], hs[1][:], spent[:, 0:HALF]]
         for u in range(ROW_BLOCKS):
-            recall(u, 1, late[u % 2])
-        put_features(0, *x_first)
-        put_features(1, *quantise_x(1))
+            recall(u, 1, late[u])
+        put_features(0, [(0, banks[2]), (1, banks[3])], *x_first)
+        spent, x_second = quantise_x(1)
+        put_features(0, [(2, banks[1])], *x_first)
+        put_features(1, [(0, banks[0]), (1, banks[2]), (2, banks[3])], *x_second)

@@ -168,7 +168,10 @@ def tile_list_latex_tapping_roster_kernel(
         hs = [held(f"h{s}", [P, HALF], F32) for s in range(2)]
 
         def scale_wgs(u, half):
-            nc.scalar.activation(wg[u % 2][half][:], wgs_sb[half][:], ACT.Copy, scale=gain_col[u])
+            if u == 0 and half == 0:
+                nc.vector.tensor_scalar(wg[0][0][:], wgs_sb[0][:], gain_col[0], None, ALU.mult)
+            else:
+                nc.scalar.activation(wg[u % 2][half][:], wgs_sb[half][:], ACT.Copy, scale=gain_col[u])
 
         def products(u, half):
             ac = banks[2 * half : 2 * half + 2]
@@ -178,25 +181,31 @@ def tile_list_latex_tapping_roster_kernel(
                 cols = slice(P * jb, P * (jb + 1))
                 return v_codes[a][half][:, cols].bitcast(FP8X4), cols
 
-            for a in range(PASSES):
-                for jb in range(JB):
-                    lhs, cols = entries(a, jb)
-                    nc.tensor.matmul_mx(
-                        out=ac[jb // 2][:, 2 * P * (jb % 2) : 2 * P * (jb % 2 + 1)],
-                        lhsT=lhs, lhsT_scale=v_planes[half][4 * a : P, cols],
-                        rhs=w_codes[u][a][:].bitcast(FP8X4), rhs_scale=w_plane[u][a][:],
-                        start=(a == 0 and jb % 2 == 0), stop=(a == PASSES - 1 and jb % 2 == 1),
-                    )
-            for a in range(PASSES):
-                for jb in range(JB):
-                    lhs, cols = entries(a, jb)
-                    nc.tensor.matmul_mx(
-                        out=b_bank[:, jb, :],
-                        lhsT=lhs, lhsT_scale=v_plane[a][half][:, cols],
-                        rhs=wb_codes[:, a, 2 * P * u : 2 * P * (u + 1)].bitcast(FP4X4),
-                        rhs_scale=wb_planes[:, a, P * u : P * (u + 1)],
-                        start=(a == 0 and jb == 0), stop=(a == PASSES - 1 and jb == JB - 1),
-                    )
+            def a_and_c():
+                for a in range(PASSES):
+                    for jb in range(JB):
+                        lhs, cols = entries(a, jb)
+                        nc.tensor.matmul_mx(
+                            out=ac[jb // 2][:, 2 * P * (jb % 2) : 2 * P * (jb % 2 + 1)],
+                            lhsT=lhs, lhsT_scale=v_planes[half][4 * a : P, cols],
+                            rhs=w_codes[u][a][:].bitcast(FP8X4), rhs_scale=w_plane[u][a][:],
+                            start=(a == 0 and jb % 2 == 0), stop=(a == PASSES - 1 and jb % 2 == 1),
+                        )
+
+            def b_alone():
+                for a in range(PASSES):
+                    for jb in range(JB):
+                        lhs, cols = entries(a, jb)
+                        nc.tensor.matmul_mx(
+                            out=b_bank[:, jb, :],
+                            lhsT=lhs, lhsT_scale=v_plane[a][half][:, cols],
+                            rhs=wb_codes[:, a, 2 * P * u : 2 * P * (u + 1)].bitcast(FP4X4),
+                            rhs_scale=wb_planes[:, a, P * u : P * (u + 1)],
+                            start=(a == 0 and jb == 0), stop=(a == PASSES - 1 and jb == JB - 1),
+                        )
+
+            for group in (a_and_c, b_alone) if u == 0 else (b_alone, a_and_c):
+                group()
             ac_sb = ring.tile([P, 2, JB, P], F32, name="ac_sb", bufs=3)
             for pair in range(2):
                 nc.scalar.copy(
@@ -223,8 +232,9 @@ def tile_list_latex_tapping_roster_kernel(
 
         def recall(u, half, picked):
             nc.vector.tensor_copy(picked, pages[u][:].indirect(half_list(idx3, half)))
-            lifted = ring.tile([P, HALF], BF16, name="lifted")
-            nc.vector.tensor_scalar(lifted[:], picked, base_col[u], None, ALU.max)
+
+        def lift(u, half, picked, lifted):
+            nc.vector.tensor_scalar(lifted, picked, base_col[u], None, ALU.max)
             turned = psum.tile([P, JB, P], BF16, name="turned")
             for jb in range(JB):
                 nc.tensor.transpose(turned[:, jb, :], lifted[:, P * jb : P * (jb + 1)], ident_bf[:])
@@ -272,12 +282,16 @@ def tile_list_latex_tapping_roster_kernel(
         gather_table(1, 0)
         gather_table(1, 1)
         steps = [(u, half) for u in range(ROW_BLOCKS) for half in range(2)]
+
+        def a_part(step):
+            return step[0][:, 0].rearrange("p b r -> p (b r)")
+
         ahead = products(*steps[0])
         for i, (u, half) in enumerate(steps):
             now = ahead
             scale_wgs(u, half)
             last = i + 1 == len(steps)
-            takes_weights = u + 1 < ROW_BLOCKS and half == (1 if u == 0 else 0)
+            takes_weights = u + 1 < ROW_BLOCKS and half == (1 if u < 2 else 0)
             if takes_weights:
                 quantise_weights(u + 1)
             if not last:
@@ -286,14 +300,27 @@ def tile_list_latex_tapping_roster_kernel(
                 state = raw[u + 1][1][:, 0].rearrange("p j c -> p (j c)")
             else:
                 state = hs[half][:]
+            if half == 0 and u > 0:
+                lift(u - 1, 0, a_part(now), a_part(ahead).bitcast(BF16)[:, 0:HALF])
             put_states(u, half, state, *now)
-            if half == 1:
-                recall(u, 0, hs[0][:] if last else ahead[0][:, 0].rearrange("p b r -> p (b r)"))
+            if half == 1 and not last:
+                recall(u, 0, a_part(ahead))
 
+        def lift_late(u, half, picked):
+            lifted = ring.tile([P, HALF], BF16, name="lifted")
+            lift(u, half, picked, lifted[:])
+
+        recall(3, 0, hs[0][:])
+        recall(0, 1, hs[1][:])
+        lift_late(3, 0, hs[0][:])
         spent, x_first = quantise_x(0)
-        late = [hs[1][:], wg[1][1][:], hs[1][:], spent[:, 0:HALF]]
-        for u in range(ROW_BLOCKS):
-            recall(u, 1, late[u])
+        recall(1, 1, wg[1][1][:])
+        lift_late(0, 1, hs[1][:])
+        recall(2, 1, hs[0][:])
+        lift_late(1, 1, wg[1][1][:])
+        recall(3, 1, spent[:, 0:HALF])
+        lift_late(2, 1, hs[0][:])
+        lift_late(3, 1, spent[:, 0:HALF])
         put_features(0, [(0, banks[2]), (1, banks[3])], *x_first)
         spent, x_second = quantise_x(1)
         put_features(0, [(2, banks[1])], *x_first)

@@ -18,12 +18,20 @@ ACT = mybir.ActivationFunctionType
 ALU = mybir.AluOpType
 
 P = 128
-PASSES = K // 512
+PACK = 4
+K_PASS = P * PACK
+PASSES = K // K_PASS
+QUADRANTS = 4
+QUAD = P // QUADRANTS
+SCALE_ROWS = 4
 ROW_BLOCKS = H // P
 OUT_BLOCKS = N // P
 HALF = 512
+HALVES = S // HALF
 LIST_COLS = HALF // 16
 JB = HALF // P
+LAST_ROW = QUAD * (QUADRANTS - 1) + SCALE_ROWS
+EARLY_FROM = 2
 
 
 def tile_list_latex_tapping_roster_kernel(
@@ -40,10 +48,10 @@ def tile_list_latex_tapping_roster_kernel(
         def held(name, shape, dtype):
             return keep.tile(shape, dtype, name=name, align_bytes=64)
 
-        banks = [psum.tile([P, HALF], F32, name=f"bank{i}") for i in range(4)]
-
         def half_list(tile, half):
             return tile[:, half * LIST_COLS : (half + 1) * LIST_COLS]
+
+        banks = [psum.tile([P, HALF], F32, name=f"bank{i}") for i in range(4)]
 
         idx = lists.tile([P, S // 16], U16, name="idx")
         idx2 = lists.tile([P, S // 16], U16, name="idx2")
@@ -54,21 +62,16 @@ def tile_list_latex_tapping_roster_kernel(
         nc.vector.memset(tab_planes[:].bitcast(I32), 0)
         wb_planes = held("wb_planes", [P, PASSES, H], U8)
         nc.vector.memset(wb_planes[:].rearrange("p a c -> p (a c)").bitcast(I32), 0)
-        v_plane1 = [held(f"v_plane1_{h}", [P, HALF], U8) for h in range(2)]
-        for h in range(2):
-            nc.vector.memset(v_plane1[h][96:P, :].bitcast(I32), 0)
+        v_plane_moved = [held(f"v_plane_moved{half}", [P, HALF], U8) for half in range(HALVES)]
+        for half in range(HALVES):
+            nc.vector.memset(v_plane_moved[half][P - QUAD : P, :].bitcast(I32), 0)
         ident = held("ident", [P, P], F32)
         make_identity(nc, ident[:])
         w4_plane = held("w4_plane", [P, N], U8)
         nc.vector.memset(w4_plane[:].bitcast(I32), 0)
 
-        warm = held("warm", [P, 1], F32)
-        nc.scalar.activation(warm[:], ident[:, 0:1], ACT.Tanh)
-
-
-        nc.sync.dma_start(idx[:], offs)
         table = [held(f"table{a}", [P, T], U32) for a in range(PASSES)]
-        raw = [[held(f"raw{u}_{a}", [P, 2, 4, P], F32) for a in range(PASSES)] for u in range(ROW_BLOCKS)]
+        raw = [[held(f"raw{u}_{a}", [P, 2, PACK, P], F32) for a in range(PASSES)] for u in range(ROW_BLOCKS)]
         pages = [held(f"page{u}", [P, T2], F32) for u in range(ROW_BLOCKS)]
         outs = [held(f"out{n}", [P, T2], F32) for n in range(OUT_BLOCKS)]
 
@@ -78,24 +81,11 @@ def tile_list_latex_tapping_roster_kernel(
         def load_weights(u):
             for a in range(PASSES):
                 for w, weight in enumerate((wa, wc)):
-                    rows = weight[512 * a : 512 * (a + 1), P * u : P * (u + 1)]
-                    nc.sync.dma_start(raw[u][a][:, w], rows.rearrange("(p j) c -> p j c", j=4))
+                    rows = weight[K_PASS * a : K_PASS * (a + 1), P * u : P * (u + 1)]
+                    nc.sync.dma_start(raw[u][a][:, w], rows.rearrange("(p t) c -> p t c", t=PACK))
 
-        load_table(0)
-        for q in range(4):
-            nc.sync.dma_start(
-                tab_planes[32 * q : 32 * q + 8, :].bitcast(I32),
-                tab_scales[:, 4 * q : 4 * q + 4, :].bitcast(I32),
-            )
-        load_weights(0)
-        load_table(1)
-        wb_codes = held("wb_codes", [P, PASSES, 2 * H], U8)
-        nc.sync.dma_start(wb_codes[:].bitcast(I32), wb_words.rearrange("a p c -> p a c").bitcast(I32))
-        for q in range(4):
-            nc.sync.dma_start(
-                wb_planes[32 * q : 32 * q + 4, :, :].bitcast(I32),
-                wb_scales[:, 4 * q : 4 * q + 4, :].rearrange("a r c -> r a c").bitcast(I32),
-            )
+        def load_page(u):
+            nc.sync.dma_start(pages[u][:], page0[P * u : P * (u + 1), :])
 
         def load_columns(name, vector, first, count):
             tile = held(name, [P, count], F32)
@@ -103,27 +93,43 @@ def tile_list_latex_tapping_roster_kernel(
                 nc.sync.dma_start(tile[:], vector.rearrange("(u p) -> p u", p=P)[:, first : first + count])
             return [tile[:, u : u + 1] for u in range(count)]
 
+        nc.sync.dma_start(idx[:], offs)
+        load_table(0)
+        for q in range(QUADRANTS):
+            nc.sync.dma_start(
+                tab_planes[QUAD * q : QUAD * q + PASSES * SCALE_ROWS, :].bitcast(I32),
+                tab_scales[:, SCALE_ROWS * q : SCALE_ROWS * (q + 1), :].bitcast(I32),
+            )
+        load_weights(0)
+        load_table(1)
+        wb_codes = held("wb_codes", [P, PASSES, 2 * H], U8)
+        nc.sync.dma_start(wb_codes[:].bitcast(I32), wb_words.rearrange("a p c -> p a c").bitcast(I32))
+        for q in range(QUADRANTS):
+            nc.sync.dma_start(
+                wb_planes[QUAD * q : QUAD * q + SCALE_ROWS, :, :].bitcast(I32),
+                wb_scales[:, SCALE_ROWS * q : SCALE_ROWS * (q + 1), :].rearrange("a r c -> r a c").bitcast(I32),
+            )
         gain_col = load_columns("gain_first", gain, 0, 1)
-        wgs_sb = [held(f"wgs{h}", [P, HALF], F32) for h in range(2)]
+        wgs_sb = [held(f"wgs{half}", [P, HALF], F32) for half in range(HALVES)]
         nc.sync.dma_start(wgs_sb[0][:], wgs[:, 0:HALF])
         nc.sync.dma_start(idx2[:], offs2)
-        nc.sync.dma_start(pages[0][:], page0[0:P, :])
+        load_page(0)
         nc.sync.dma_start(wgs_sb[1][:], wgs[:, HALF:S])
         load_weights(1)
         nc.sync.dma_start(idx3[:], offs3)
         gain_col = gain_col + load_columns("gain_rest", gain, 1, ROW_BLOCKS - 1)
         base_col = load_columns("base_cols", base, 0, ROW_BLOCKS)
-        nc.sync.dma_start(pages[1][:], page0[P : 2 * P, :])
+        load_page(1)
         for u in range(2, ROW_BLOCKS):
             load_weights(u)
-            nc.sync.dma_start(pages[u][:], page0[P * u : P * (u + 1), :])
+            load_page(u)
         thr_col = load_columns("thr_cols", thr, 0, OUT_BLOCKS)
         w4_codes = held("w4_codes", [P, N], U32)
         nc.sync.dma_start(w4_codes[:].bitcast(I32), w4_words[0].rearrange("p c i -> p (c i)").bitcast(I32))
-        for q in range(4):
+        for q in range(QUADRANTS):
             nc.sync.dma_start(
-                w4_plane[32 * q : 32 * q + 4, :].bitcast(I32),
-                w4_scales[0, 4 * q : 4 * q + 4, :].bitcast(I32),
+                w4_plane[QUAD * q : QUAD * q + SCALE_ROWS, :].bitcast(I32),
+                w4_scales[0, SCALE_ROWS * q : SCALE_ROWS * (q + 1), :].bitcast(I32),
             )
         nc.sync.dma_start(idx4[:], offs4)
         wgo_sb = held("wgo_sb", [P, PICK], F32)
@@ -131,17 +137,21 @@ def tile_list_latex_tapping_roster_kernel(
         for n in range(OUT_BLOCKS):
             nc.sync.dma_start(outs[n][:], page1[P * n : P * (n + 1), :])
 
-        v_planes = [held(f"v_planes{h}", [P, HALF], U8) for h in range(2)]
-        v_plane = [v_planes, v_plane1]
+        v_planes = [held(f"v_planes{half}", [P, HALF], U8) for half in range(HALVES)]
 
         def gather_scales(half):
             nc.vector.tensor_copy(v_planes[half][:], tab_planes[:].indirect(half_list(idx, half)))
-            nc.scalar.dma_start(v_plane1[half][0:112, :].bitcast(I32), v_planes[half][4:116, :].bitcast(I32))
+            nc.scalar.dma_start(
+                v_plane_moved[half][0:LAST_ROW, :].bitcast(I32),
+                v_planes[half][SCALE_ROWS : SCALE_ROWS + LAST_ROW, :].bitcast(I32),
+            )
+
+        v_plane_from_row0 = [v_planes, v_plane_moved]
 
         ident_bf = held("ident_bf", [P, P], BF16)
         make_identity(nc, ident_bf[:])
 
-        v_codes = [[held(f"v_codes{a}_{h}", [P, HALF], U32) for h in range(2)] for a in range(PASSES)]
+        v_codes = [[held(f"v_codes{a}_{half}", [P, HALF], U32) for half in range(HALVES)] for a in range(PASSES)]
 
         def gather_table(a, half):
             nc.vector.tensor_copy(v_codes[a][half][:], table[a][:].indirect(half_list(idx, half)))
@@ -151,21 +161,22 @@ def tile_list_latex_tapping_roster_kernel(
 
         def quantise_weights(u):
             for a in range(PASSES):
-                grouped = ring.tile([P, 2, P, 4], BF16, name="grouped", align_bytes=64, bufs=3)
-                dst = grouped[:].rearrange("p w (c i) j -> p w c j i", i=4)
-                src = raw[u][a][:].rearrange("p w j (c i) -> p w c j i", i=4)
-                if u == 0:
-                    nc.vector.tensor_copy(dst, src)
-                else:
-                    nc.scalar.copy(dst, src)
+                grouped = ring.tile([P, 2, P, PACK], BF16, name="grouped", align_bytes=64, bufs=3)
+                dst = grouped[:].rearrange("p w (c i) t -> p w c t i", i=4)
+                src = raw[u][a][:].rearrange("p w t (c i) -> p w c t i", i=4)
+                for w in range(2):
+                    if u == 0:
+                        nc.vector.tensor_copy(dst[:, w], src[:, w])
+                    else:
+                        nc.scalar.copy(dst[:, w], src[:, w])
                 nc.vector.quantize_mx(
                     out=w_codes[u][a][:].bitcast(FP8X4),
                     scales=w_plane[u][a][:],
-                    in_=grouped[:].rearrange("p w c j -> p (w c j)"),
+                    in_=grouped[:].rearrange("p w c t -> p (w c t)"),
                 )
 
-        wg = [[held(f"wg{s}_{h}", [P, HALF], F32) for h in range(2)] for s in range(2)]
-        hs = [held(f"h{s}", [P, HALF], F32) for s in range(2)]
+        wg = [[held(f"wg{s}_{half}", [P, HALF], F32) for half in range(HALVES)] for s in range(2)]
+        states = [held(f"state{half}", [P, HALF], F32) for half in range(HALVES)]
 
         def scale_wgs(u, half):
             if u == 0 and half == 0:
@@ -174,20 +185,20 @@ def tile_list_latex_tapping_roster_kernel(
                 nc.scalar.activation(wg[u % 2][half][:], wgs_sb[half][:], ACT.Copy, scale=gain_col[u])
 
         def products(u, half):
-            ac = banks[2 * half : 2 * half + 2]
+            ad_banks = banks[2 * half : 2 * half + 2]
             b_bank = psum.tile([P, JB, P], F32, name="b_bank", bufs=2)
 
             def entries(a, jb):
                 cols = slice(P * jb, P * (jb + 1))
                 return v_codes[a][half][:, cols].bitcast(FP8X4), cols
 
-            def a_and_c():
+            def a_and_d():
                 for a in range(PASSES):
                     for jb in range(JB):
                         lhs, cols = entries(a, jb)
                         nc.tensor.matmul_mx(
-                            out=ac[jb // 2][:, 2 * P * (jb % 2) : 2 * P * (jb % 2 + 1)],
-                            lhsT=lhs, lhsT_scale=v_planes[half][4 * a : P, cols],
+                            out=ad_banks[jb // 2][:, 2 * P * (jb % 2) : 2 * P * (jb % 2 + 1)],
+                            lhsT=lhs, lhsT_scale=v_planes[half][SCALE_ROWS * a : P, cols],
                             rhs=w_codes[u][a][:].bitcast(FP8X4), rhs_scale=w_plane[u][a][:],
                             start=(a == 0 and jb % 2 == 0), stop=(a == PASSES - 1 and jb % 2 == 1),
                         )
@@ -198,37 +209,37 @@ def tile_list_latex_tapping_roster_kernel(
                         lhs, cols = entries(a, jb)
                         nc.tensor.matmul_mx(
                             out=b_bank[:, jb, :],
-                            lhsT=lhs, lhsT_scale=v_plane[a][half][:, cols],
+                            lhsT=lhs, lhsT_scale=v_plane_from_row0[a][half][:, cols],
                             rhs=wb_codes[:, a, 2 * P * u : 2 * P * (u + 1)].bitcast(FP4X4),
                             rhs_scale=wb_planes[:, a, P * u : P * (u + 1)],
                             start=(a == 0 and jb == 0), stop=(a == PASSES - 1 and jb == JB - 1),
                         )
 
-            for group in (a_and_c, b_alone) if u == 0 else (b_alone, a_and_c):
+            for group in (a_and_d, b_alone) if u == 0 else (b_alone, a_and_d):
                 group()
-            ac_sb = ring.tile([P, 2, JB, P], F32, name="ac_sb", bufs=3)
+            ad_sb = ring.tile([P, 2, JB, P], F32, name="ad_sb", bufs=3)
             for pair in range(2):
                 nc.scalar.copy(
-                    ac_sb[:, :, 2 * pair : 2 * pair + 2, :],
-                    ac[pair][:].rearrange("p (b w r) -> p w b r", b=2, w=2),
+                    ad_sb[:, :, 2 * pair : 2 * pair + 2, :],
+                    ad_banks[pair][:].rearrange("p (b w r) -> p w b r", b=2, w=2),
                 )
             ab = ring.tile([P, JB, P], F32, name="ab")
-            nc.vector.tensor_tensor(ab[:], b_bank[:], ac_sb[:, 0], ALU.mult)
-            return ac_sb, ab
+            nc.vector.tensor_tensor(ab[:], b_bank[:], ad_sb[:, 0], ALU.mult)
+            return ad_sb, ab
 
-        def put_states(u, half, state, ac_sb, ab):
+        def put_states(u, half, state, ad_sb, ab):
             total = psum.tile([P, JB, P], F32, name="total")
             for jb in range(JB):
-                nc.tensor.matmul(total[:, jb, :], ac_sb[:, 1, jb, :], ident[:], start=(jb == 0), stop=False, is_transpose=True)
+                nc.tensor.matmul(total[:, jb, :], ad_sb[:, 1, jb, :], ident[:], start=(jb == 0), stop=False, is_transpose=True)
             for jb in range(JB):
                 nc.tensor.matmul(total[:, jb, :], ab[:, jb, :], ident[:], start=False, stop=(jb == JB - 1), is_transpose=True)
-            nc.scalar.activation(state, total[:].rearrange("p b r -> p (b r)"), ACT.Tanh)
+            nc.scalar.activation(state, total[:].rearrange("p b j -> p (b j)"), ACT.Tanh)
             nc.vector.tensor_tensor(
                 pages[u][:].indirect(half_list(idx2, half)),
                 state, wg[u % 2][half][:], ALU.mult,
             )
 
-        x_t = [held(f"x_t{h}", [P, JB, H], BF16) for h in range(2)]
+        x_t = [held(f"x_t{half}", [P, JB, 2, P], F32) for half in range(HALVES)]
 
         def recall(u, half, picked):
             nc.vector.tensor_copy(picked, pages[u][:].indirect(half_list(idx3, half)))
@@ -238,17 +249,19 @@ def tile_list_latex_tapping_roster_kernel(
             turned = psum.tile([P, JB, P], BF16, name="turned")
             for jb in range(JB):
                 nc.tensor.transpose(turned[:, jb, :], lifted[:, P * jb : P * (jb + 1)], ident_bf[:])
-            nc.scalar.copy(x_t[half][:, :, P * u : P * (u + 1)], turned[:])
+            nc.scalar.copy(
+                x_t[half][:, :, :, QUAD * u : QUAD * (u + 1)],
+                turned[:].bitcast(F32).rearrange("j b (q e) -> j b e q", e=2),
+            )
 
         def quantise_x(half):
-            x_grouped = ring.tile([P, 4 * HALF], BF16, name="x_grouped", align_bytes=64)
+            x_grouped = ring.tile([P, PACK * HALF], BF16, name="x_grouped", align_bytes=64)
             x_words = x_grouped[:].bitcast(F32)
             for pair in range(2):
                 back = banks[pair]
                 for b in range(2):
-                    words = x_t[half][:, 2 * pair + b, :].bitcast(F32)
                     for e in range(2):
-                        nc.tensor.transpose(back[:, P * (2 * b + e) : P * (2 * b + e + 1)], words[:, e : 2 * P : 2], ident[:])
+                        nc.tensor.transpose(back[:, P * (2 * b + e) : P * (2 * b + e + 1)], x_t[half][:, 2 * pair + b, e, :], ident[:])
                 nc.scalar.copy(
                     x_words[:, HALF * pair : HALF * (pair + 1)].rearrange("p (b j e) -> p b j e", b=2, e=2),
                     back[:].rearrange("p (b e j) -> p b j e", b=2, e=2),
@@ -266,22 +279,22 @@ def tile_list_latex_tapping_roster_kernel(
                     rhs=x_codes[:].bitcast(FP8X4), rhs_scale=x_plane[:],
                     start=True, stop=True,
                 )
-                y = ring.tile([P, HALF], F32, name="y", bufs=3)
+                y = ring.tile([P, HALF], F32, name="y", bufs=OUT_BLOCKS)
                 nc.scalar.activation(y[:], y_bank[:], ACT.Abs, bias=thr_col[n], scale=-1.0)
                 nc.vector.tensor_tensor(
                     outs[n][:].indirect(half_list(idx4, half)),
                     y[:], wgo_sb[:, HALF * half : HALF * (half + 1)], ALU.mult,
                 )
-                if half == 1:
+                if half == HALVES - 1:
                     nc.sync.dma_start(out[P * n : P * (n + 1), :], outs[n][:])
 
-        for half in range(2):
+        for half in range(HALVES):
             gather_scales(half)
             gather_table(0, half)
         quantise_weights(0)
-        gather_table(1, 0)
-        gather_table(1, 1)
-        steps = [(u, half) for u in range(ROW_BLOCKS) for half in range(2)]
+        for half in range(HALVES):
+            gather_table(1, half)
+        steps = [(u, half) for u in range(ROW_BLOCKS) for half in range(HALVES)]
 
         def a_part(step):
             return step[0][:, 0].rearrange("p b r -> p (b r)")
@@ -291,15 +304,15 @@ def tile_list_latex_tapping_roster_kernel(
             now = ahead
             scale_wgs(u, half)
             last = i + 1 == len(steps)
-            takes_weights = u + 1 < ROW_BLOCKS and half == (1 if u < 2 else 0)
+            takes_weights = u + 1 < ROW_BLOCKS and half == (1 if u < EARLY_FROM else 0)
             if takes_weights:
                 quantise_weights(u + 1)
             if not last:
                 ahead = products(*steps[i + 1])
             if takes_weights:
-                state = raw[u + 1][1][:, 0].rearrange("p j c -> p (j c)")
+                state = raw[u + 1][PASSES - 1][:, 0].rearrange("p t c -> p (t c)")
             else:
-                state = hs[half][:]
+                state = states[half][:]
             if half == 0 and u > 0:
                 lift(u - 1, 0, a_part(now), a_part(ahead).bitcast(BF16)[:, 0:HALF])
             put_states(u, half, state, *now)
@@ -310,18 +323,17 @@ def tile_list_latex_tapping_roster_kernel(
             lifted = ring.tile([P, HALF], BF16, name="lifted")
             lift(u, half, picked, lifted[:])
 
-        recall(3, 0, hs[0][:])
-        recall(0, 1, hs[1][:])
-        lift_late(3, 0, hs[0][:])
-        spent, x_first = quantise_x(0)
-        recall(1, 1, wg[1][1][:])
-        lift_late(0, 1, hs[1][:])
-        recall(2, 1, hs[0][:])
-        lift_late(1, 1, wg[1][1][:])
-        recall(3, 1, spent[:, 0:HALF])
-        lift_late(2, 1, hs[0][:])
-        lift_late(3, 1, spent[:, 0:HALF])
+        end = ROW_BLOCKS - 1
+        recall(end, 0, states[0][:])
+        lift_late(end, 0, states[0][:])
+        spent_words, x_first = quantise_x(0)
+        rooms = [states[1][:], wg[end % 2][1][:], states[0][:], spent_words[:, 0:HALF]]
+        for u in range(ROW_BLOCKS):
+            recall(u, 1, rooms[u])
+            if u > 0:
+                lift_late(u - 1, 1, rooms[u - 1])
+        lift_late(end, 1, rooms[end])
         put_features(0, [(0, banks[2]), (1, banks[3])], *x_first)
-        spent, x_second = quantise_x(1)
+        x_second = quantise_x(1)[1]
         put_features(0, [(2, banks[1])], *x_first)
         put_features(1, [(0, banks[0]), (1, banks[2]), (2, banks[3])], *x_second)

from contextlib import ExitStack

import concourse.mybir as mybir
from concourse.masks import make_identity

K, T, S, H, T2, PICK, N = 1024, 4096, 1024, 512, 2048, 1024, 384
FLOPS = 2 * (3 * K * H * S + H * N * PICK)

F32 = mybir.dt.float32
BF16 = mybir.dt.bfloat16
I32 = mybir.dt.int32
U32 = mybir.dt.uint32
U16 = mybir.dt.uint16
U8 = mybir.dt.uint8
FP8X4 = mybir.dt.float8_e4m3fn_x4
FP4X4 = mybir.dt.float4_e2m1fn_x4
ACT = mybir.ActivationFunctionType
ALU = mybir.AluOpType

P = 128
PACK = 4
K_PASS = P * PACK
PASSES = K // K_PASS
QUADRANTS = 4
QUAD = P // QUADRANTS
SCALE_ROWS = 4
ROW_BLOCKS = H // P
OUT_BLOCKS = N // P
HALF = 512
HALVES = S // HALF
LIST_COLS = HALF // 16
JB = HALF // P
LAST_ROW = QUAD * (QUADRANTS - 1) + SCALE_ROWS
EARLY_FROM = 2


def tile_list_latex_tapping_roster_kernel(
    tc, tab_words, tab_scales, offs, wa, wb_words, wb_scales, wc, gain, wgs, page0, offs2, offs3,
    base, w4_words, w4_scales, thr, wgo, page1, offs4, out,
):
    nc = tc.nc
    with ExitStack() as ctx:
        lists = ctx.enter_context(tc.tile_pool(name="lists", bufs=1))
        keep = ctx.enter_context(tc.tile_pool(name="keep", bufs=1))
        ring = ctx.enter_context(tc.tile_pool(name="ring", bufs=2))
        psum = ctx.enter_context(tc.psum_pool(name="psum", bufs=1))

        def held(name, shape, dtype):
            return keep.tile(shape, dtype, name=name, align_bytes=64)

        def half_list(tile, half):
            return tile[:, half * LIST_COLS : (half + 1) * LIST_COLS]

        banks = [psum.tile([P, HALF], F32, name=f"bank{i}") for i in range(4)]

        idx = lists.tile([P, S // 16], U16, name="idx")
        idx2 = lists.tile([P, S // 16], U16, name="idx2")
        idx3 = lists.tile([P, PICK // 16], U16, name="idx3")
        idx4 = lists.tile([P, PICK // 16], U16, name="idx4")

        tab_planes = held("tab_planes", [P, T], U8)
        nc.vector.memset(tab_planes[:].bitcast(I32), 0)
        wb_planes = held("wb_planes", [P, PASSES, H], U8)
        nc.vector.memset(wb_planes[:].rearrange("p a c -> p (a c)").bitcast(I32), 0)
        v_plane_moved = [held(f"v_plane_moved{half}", [P, HALF], U8) for half in range(HALVES)]
        for half in range(HALVES):
            nc.vector.memset(v_plane_moved[half][P - QUAD : P, :].bitcast(I32), 0)
        ident = held("ident", [P, P], F32)
        make_identity(nc, ident[:])
        w4_plane = held("w4_plane", [P, N], U8)
        nc.vector.memset(w4_plane[:].bitcast(I32), 0)

        table = [held(f"table{a}", [P, T], U32) for a in range(PASSES)]
        raw = [[held(f"raw{u}_{a}", [P, 2, PACK, P], F32) for a in range(PASSES)] for u in range(ROW_BLOCKS)]
        pages = [held(f"page{u}", [P, T2], F32) for u in range(ROW_BLOCKS)]
        outs = [held(f"out{n}", [P, T2], F32) for n in range(OUT_BLOCKS)]

        def load_table(a):
            nc.sync.dma_start(table[a][:].bitcast(I32), tab_words[a].rearrange("p t i -> p (t i)").bitcast(I32))

        def load_weights(u):
            for a in range(PASSES):
                for w, weight in enumerate((wa, wc)):
                    rows = weight[K_PASS * a : K_PASS * (a + 1), P * u : P * (u + 1)]
                    nc.sync.dma_start(raw[u][a][:, w], rows.rearrange("(p t) c -> p t c", t=PACK))

        def load_page(u):
            nc.sync.dma_start(pages[u][:], page0[P * u : P * (u + 1), :])

        def load_columns(name, vector, first, count):
            tile = held(name, [P, count], F32)
            with nc.allow_non_contiguous_dma(reason="one value of a short vector for each partition"):
                nc.sync.dma_start(tile[:], vector.rearrange("(u p) -> p u", p=P)[:, first : first + count])
            return [tile[:, u : u + 1] for u in range(count)]

        nc.sync.dma_start(idx[:], offs)
        load_table(0)
        for q in range(QUADRANTS):
            nc.sync.dma_start(
                tab_planes[QUAD * q : QUAD * q + PASSES * SCALE_ROWS, :].bitcast(I32),
                tab_scales[:, SCALE_ROWS * q : SCALE_ROWS * (q + 1), :].bitcast(I32),
            )
        load_weights(0)
        load_table(1)
        wb_codes = held("wb_codes", [P, PASSES, 2 * H], U8)
        nc.sync.dma_start(wb_codes[:].bitcast(I32), wb_words.rearrange("a p c -> p a c").bitcast(I32))
        for q in range(QUADRANTS):
            nc.sync.dma_start(
                wb_planes[QUAD * q : QUAD * q + SCALE_ROWS, :, :].bitcast(I32),
                wb_scales[:, SCALE_ROWS * q : SCALE_ROWS * (q + 1), :].rearrange("a r c -> r a c").bitcast(I32),
            )
        gain_col = load_columns("gain_first", gain, 0, 1)
        wgs_sb = [held(f"wgs{half}", [P, HALF], F32) for half in range(HALVES)]
        nc.sync.dma_start(wgs_sb[0][:], wgs[:, 0:HALF])
        nc.sync.dma_start(idx2[:], offs2)
        load_page(0)
        nc.sync.dma_start(wgs_sb[1][:], wgs[:, HALF:S])
        load_weights(1)
        nc.sync.dma_start(idx3[:], offs3)
        gain_col = gain_col + load_columns("gain_rest", gain, 1, ROW_BLOCKS - 1)
        base_col = load_columns("base_cols", base, 0, ROW_BLOCKS)
        load_page(1)
        for u in range(2, ROW_BLOCKS):
            load_weights(u)
            load_page(u)
        thr_col = load_columns("thr_cols", thr, 0, OUT_BLOCKS)
        w4_codes = held("w4_codes", [P, N], U32)
        nc.sync.dma_start(w4_codes[:].bitcast(I32), w4_words[0].rearrange("p c i -> p (c i)").bitcast(I32))
        for q in range(QUADRANTS):
            nc.sync.dma_start(
                w4_plane[QUAD * q : QUAD * q + SCALE_ROWS, :].bitcast(I32),
                w4_scales[0, SCALE_ROWS * q : SCALE_ROWS * (q + 1), :].bitcast(I32),
            )
        nc.sync.dma_start(idx4[:], offs4)
        wgo_sb = held("wgo_sb", [P, PICK], F32)
        nc.sync.dma_start(wgo_sb[:], wgo)
        for n in range(OUT_BLOCKS):
            nc.sync.dma_start(outs[n][:], page1[P * n : P * (n + 1), :])

        v_planes = [held(f"v_planes{half}", [P, HALF], U8) for half in range(HALVES)]

        def gather_scales(half):
            nc.vector.tensor_copy(v_planes[half][:], tab_planes[:].indirect(half_list(idx, half)))
            nc.scalar.dma_start(
                v_plane_moved[half][0:LAST_ROW, :].bitcast(I32),
                v_planes[half][SCALE_ROWS : SCALE_ROWS + LAST_ROW, :].bitcast(I32),
            )

        v_plane_from_row0 = [v_planes, v_plane_moved]

        ident_bf = held("ident_bf", [P, P], BF16)
        make_identity(nc, ident_bf[:])

        v_codes = [[held(f"v_codes{a}_{half}", [P, HALF], U32) for half in range(HALVES)] for a in range(PASSES)]

        def gather_table(a, half):
            nc.vector.tensor_copy(v_codes[a][half][:], table[a][:].indirect(half_list(idx, half)))

        w_codes = [[held(f"w_codes{u}_{a}", [P, 2 * P], U32) for a in range(PASSES)] for u in range(ROW_BLOCKS)]
        w_plane = [[held(f"w_plane{u}_{a}", [P, 2 * P], U8) for a in range(PASSES)] for u in range(ROW_BLOCKS)]

        def quantise_weights(u):
            for a in range(PASSES):
                grouped = ring.tile([P, 2, P, PACK], BF16, name="grouped", align_bytes=64, bufs=3)
                dst = grouped[:].rearrange("p w (c i) t -> p w c t i", i=4)
                src = raw[u][a][:].rearrange("p w t (c i) -> p w c t i", i=4)
                for w in range(2):
                    if u == 0:
                        nc.vector.tensor_copy(dst[:, w], src[:, w])
                    else:
                        nc.scalar.copy(dst[:, w], src[:, w])
                nc.vector.quantize_mx(
                    out=w_codes[u][a][:].bitcast(FP8X4),
                    scales=w_plane[u][a][:],
                    in_=grouped[:].rearrange("p w c t -> p (w c t)"),
                )

        wg = [[held(f"wg{s}_{half}", [P, HALF], F32) for half in range(HALVES)] for s in range(2)]
        states = [held(f"state{half}", [P, HALF], F32) for half in range(HALVES)]

        def scale_wgs(u, half):
            if u == 0 and half == 0:
                nc.vector.tensor_scalar(wg[0][0][:], wgs_sb[0][:], gain_col[0], None, ALU.mult)
            else:
                nc.scalar.activation(wg[u % 2][half][:], wgs_sb[half][:], ACT.Copy, scale=gain_col[u])

        def products(u, half):
            ad_banks = banks[2 * half : 2 * half + 2]
            b_bank = psum.tile([P, JB, P], F32, name="b_bank", bufs=2)

            def entries(a, jb):
                cols = slice(P * jb, P * (jb + 1))
                return v_codes[a][half][:, cols].bitcast(FP8X4), cols

            def a_and_d():
                for a in range(PASSES):
                    for jb in range(JB):
                        lhs, cols = entries(a, jb)
                        nc.tensor.matmul_mx(
                            out=ad_banks[jb // 2][:, 2 * P * (jb % 2) : 2 * P * (jb % 2 + 1)],
                            lhsT=lhs, lhsT_scale=v_planes[half][SCALE_ROWS * a : P, cols],
                            rhs=w_codes[u][a][:].bitcast(FP8X4), rhs_scale=w_plane[u][a][:],
                            start=(a == 0 and jb % 2 == 0), stop=(a == PASSES - 1 and jb % 2 == 1),
                        )

            def b_alone():
                for a in range(PASSES):
                    for jb in range(JB):
                        lhs, cols = entries(a, jb)
                        nc.tensor.matmul_mx(
                            out=b_bank[:, jb, :],
                            lhsT=lhs, lhsT_scale=v_plane_from_row0[a][half][:, cols],
                            rhs=wb_codes[:, a, 2 * P * u : 2 * P * (u + 1)].bitcast(FP4X4),
                            rhs_scale=wb_planes[:, a, P * u : P * (u + 1)],
                            start=(a == 0 and jb == 0), stop=(a == PASSES - 1 and jb == JB - 1),
                        )

            for group in (a_and_d, b_alone) if u == 0 else (b_alone, a_and_d):
                group()
            ad_sb = ring.tile([P, 2, JB, P], F32, name="ad_sb", bufs=3)
            for pair in range(2):
                nc.scalar.copy(
                    ad_sb[:, :, 2 * pair : 2 * pair + 2, :],
                    ad_banks[pair][:].rearrange("p (b w r) -> p w b r", b=2, w=2),
                )
            ab = ring.tile([P, JB, P], F32, name="ab")
            nc.vector.tensor_tensor(ab[:], b_bank[:], ad_sb[:, 0], ALU.mult)
            return ad_sb, ab

        def put_states(u, half, state, ad_sb, ab):
            total = psum.tile([P, JB, P], F32, name="total")
            for jb in range(JB):
                nc.tensor.matmul(total[:, jb, :], ad_sb[:, 1, jb, :], ident[:], start=(jb == 0), stop=False, is_transpose=True)
            for jb in range(JB):
                nc.tensor.matmul(total[:, jb, :], ab[:, jb, :], ident[:], start=False, stop=(jb == JB - 1), is_transpose=True)
            nc.scalar.activation(state, total[:].rearrange("p b j -> p (b j)"), ACT.Tanh)
            nc.vector.tensor_tensor(
                pages[u][:].indirect(half_list(idx2, half)),
                state, wg[u % 2][half][:], ALU.mult,
            )

        x_t = [held(f"x_t{half}", [P, JB, 2, P], F32) for half in range(HALVES)]

        def recall(u, half, picked):
            nc.vector.tensor_copy(picked, pages[u][:].indirect(half_list(idx3, half)))

        def lift(u, half, picked, lifted):
            nc.vector.tensor_scalar(lifted, picked, base_col[u], None, ALU.max)
            turned = psum.tile([P, JB, P], BF16, name="turned")
            for jb in range(JB):
                nc.tensor.transpose(turned[:, jb, :], lifted[:, P * jb : P * (jb + 1)], ident_bf[:])
            nc.scalar.copy(
                x_t[half][:, :, :, QUAD * u : QUAD * (u + 1)],
                turned[:].bitcast(F32).rearrange("j b (q e) -> j b e q", e=2),
            )

        def quantise_x(half):
            x_grouped = ring.tile([P, PACK * HALF], BF16, name="x_grouped", align_bytes=64)
            x_words = x_grouped[:].bitcast(F32)
            for pair in range(2):
                back = banks[pair]
                for b in range(2):
                    for e in range(2):
                        nc.tensor.transpose(back[:, P * (2 * b + e) : P * (2 * b + e + 1)], x_t[half][:, 2 * pair + b, e, :], ident[:])
                nc.scalar.copy(
                    x_words[:, HALF * pair : HALF * (pair + 1)].rearrange("p (b j e) -> p b j e", b=2, e=2),
                    back[:].rearrange("p (b e j) -> p b j e", b=2, e=2),
                )
            x_codes = ring.tile([P, HALF], U32, name="x_codes", align_bytes=64)
            x_plane = ring.tile([P, HALF], U8, name="x_plane", align_bytes=64)
            nc.vector.quantize_mx(out=x_codes[:].bitcast(FP8X4), scales=x_plane[:], in_=x_grouped[:])
            return x_words, (x_codes, x_plane)

        def put_features(half, blocks, x_codes, x_plane):
            for n, y_bank in blocks:
                nc.tensor.matmul_mx(
                    out=y_bank[:],
                    lhsT=w4_codes[:, P * n : P * (n + 1)].bitcast(FP8X4), lhsT_scale=w4_plane[:, P * n : P * (n + 1)],
                    rhs=x_codes[:].bitcast(FP8X4), rhs_scale=x_plane[:],
                    start=True, stop=True,
                )
                y = ring.tile([P, HALF], F32, name="y", bufs=OUT_BLOCKS)
                nc.scalar.activation(y[:], y_bank[:], ACT.Abs, bias=thr_col[n], scale=-1.0)
                nc.vector.tensor_tensor(
                    outs[n][:].indirect(half_list(idx4, half)),
                    y[:], wgo_sb[:, HALF * half : HALF * (half + 1)], ALU.mult,
                )
                if half == HALVES - 1:
                    nc.sync.dma_start(out[P * n : P * (n + 1), :], outs[n][:])

        for half in range(HALVES):
            gather_scales(half)
            gather_table(0, half)
        quantise_weights(0)
        for half in range(HALVES):
            gather_table(1, half)
        steps = [(u, half) for u in range(ROW_BLOCKS) for half in range(HALVES)]

        def a_part(step):
            return step[0][:, 0].rearrange("p b r -> p (b r)")

        ahead = products(*steps[0])
        for i, (u, half) in enumerate(steps):
            now = ahead
            scale_wgs(u, half)
            last = i + 1 == len(steps)
            takes_weights = u + 1 < ROW_BLOCKS and half == (1 if u < EARLY_FROM else 0)
            if takes_weights:
                quantise_weights(u + 1)
            if not last:
                ahead = products(*steps[i + 1])
            if takes_weights:
                state = raw[u + 1][PASSES - 1][:, 0].rearrange("p t c -> p (t c)")
            else:
                state = states[half][:]
            if half == 0 and u > 0:
                lift(u - 1, 0, a_part(now), a_part(ahead).bitcast(BF16)[:, 0:HALF])
            put_states(u, half, state, *now)
            if half == 1 and not last:
                recall(u, 0, a_part(ahead))

        def lift_late(u, half, picked):
            lifted = ring.tile([P, HALF], BF16, name="lifted")
            lift(u, half, picked, lifted[:])

        end = ROW_BLOCKS - 1
        recall(end, 0, states[0][:])
        lift_late(end, 0, states[0][:])
        spent_words, x_first = quantise_x(0)
        rooms = [states[1][:], wg[end % 2][1][:], states[0][:], spent_words[:, 0:HALF]]
        for u in range(ROW_BLOCKS):
            recall(u, 1, rooms[u])
            if u > 0:
                lift_late(u - 1, 1, rooms[u - 1])
        lift_late(end, 1, rooms[end])
        put_features(0, [(0, banks[2]), (1, banks[3])], *x_first)
        x_second = quantise_x(1)[1]
        put_features(0, [(2, banks[1])], *x_first)
        put_features(1, [(0, banks[0]), (1, banks[2]), (2, banks[3])], *x_second)
